import numpy as np
import ml_dtypes


def mxq(x, axis, fmt="e4m3"):
    dtype, down = {"e4m3": (ml_dtypes.float8_e4m3fn, 7), "e5m2": (ml_dtypes.float8_e5m2, 14)}[fmt]
    v = np.moveaxis(np.asarray(x, np.float32).astype(ml_dtypes.bfloat16).astype(np.float64), axis, -1)
    blocks = v.reshape(v.shape[:-1] + (-1, 32))
    amax = np.abs(blocks).max(-1, keepdims=True)
    byte = np.maximum(np.where(amax > 0, np.frexp(amax)[1] - 1 + 127, 0) - down, 1)
    scale = np.exp2(byte - 127.0)
    codes = (blocks / scale).astype(np.float32).astype(dtype).astype(np.float64)
    return np.moveaxis((codes * scale).reshape(v.shape), -1, axis)


WIDE = False


def mx_kscale(k, group=512):
    if not WIDE:
        return np.ones(k)
    levels = np.array([18, -18])
    if group != 512:
        return np.exp2(np.random.permutation(np.resize(levels, k // group))).repeat(group)
    if k % 512:
        return np.exp2(np.random.permutation(np.resize(levels, k // 32))).repeat(32)
    a = np.empty((k // 512, 16))
    for p in range(k // 512):
        a[p, :8] = np.random.permutation(np.resize(levels, 8))
        for g in range(8):
            far = levels[np.abs(levels - a[p, g]) >= 10]
            a[p, g + 8] = far[np.random.randint(len(far))]
    return np.exp2(a.ravel()).repeat(32)


def f64(x):
    return np.asarray(x).astype(np.float64)


def sigmoid(v):
    return 1.0 / (1.0 + np.exp(-v))


G, D, M, O, N = 4, 128, 128, 128, 512


def sgn(shape):
    return np.random.uniform(0.5, 2.0, shape) * np.where(np.random.standard_normal(shape) < 0, -1.0, 1.0)


def setup_inputs():
    n = np.random.standard_normal
    s_d = mx_kscale(D, 0)
    s_m = mx_kscale(M, 0)
    return {
        "x": (n((G, D, N)) * s_d[:, None]).astype(np.float32),
        "w1": (n((G, D, M)) / np.sqrt(D) / s_d[:, None]).astype(np.float32),
        "w2": (n((G, D, M)) / np.sqrt(D) / s_d[:, None]).astype(np.float32),
        "w3": (n((G, D, M)) / np.sqrt(D) / s_d[:, None]).astype(np.float32),
        "th": (0.5 * n((G, M, 1))).astype(np.float32),
        "hs": (sgn((G, M, 1)) * s_m[:, None]).astype(np.float32),
        "wo2": (n((G, M, O)) / np.sqrt(M) / s_m[:, None]).astype(np.float32),
        "res": (0.5 * n((G, O, N))).astype(np.float32),
    }


def reference(x, w1, w2, w3, th, hs, wo2, res):
    w1q = mxq(f64(w1), 1, "e4m3")
    xq = mxq(f64(x), 1, "e4m3")
    z1 = w1q.transpose(0, 2, 1) @ xq
    w2q = mxq(f64(w2), 1, "e4m3")
    z2 = w2q.transpose(0, 2, 1) @ xq
    w3q = mxq(f64(w3), 1, "e4m3")
    z3 = w3q.transpose(0, 2, 1) @ xq
    g2 = sigmoid(z2)
    g3 = sigmoid(z3 - f64(th))
    h = z1 * g2 * g3
    hh = h * f64(hs)
    wo2q = mxq(f64(wo2), 1, "e4m3")
    hhq = mxq(hh, 1, "e4m3")
    y0 = wo2q.transpose(0, 2, 1) @ hhq
    y = y0 + f64(res)
    return y

@@ -1,0 +1,228 @@
+from contextlib import ExitStack
+
+import concourse.mybir as mybir
+
+G, D, M, O, N = 4, 128, 128, 128, 512
+FLOPS = 2 * G * N * (3 * D * M + M * O)
+
+F32 = mybir.dt.float32
+BF16 = mybir.dt.bfloat16
+U32 = mybir.dt.uint32
+U8 = mybir.dt.uint8
+FP8X4 = mybir.dt.float8_e4m3fn_x4
+ALU = mybir.AluOpType
+ACT = mybir.ActivationFunctionType
+
+P = 128
+PACK = 4
+ROWS = 32
+NT = 128
+BANK = 512
+CHUNKS = [(0, 256), (256, 128), (384, 128)]
+
+
+def interleave(copy, dst, src):
+    copy(
+        out=dst.rearrange("p (c i) j -> p c j i", i=4),
+        in_=src.rearrange("p j (c i) -> p c j i", i=4),
+    )
+
+
+def tile_rows_ftwogates_kernel(tc, x, w1, w2, w3, th, hs, wo2, res, out):
+    nc = tc.nc
+    with ExitStack() as ctx:
+        sb = ctx.enter_context(tc.tile_pool(name="sb", bufs=1))
+        ps = ctx.enter_context(tc.psum_pool(name="ps", bufs=1))
+        ctx.enter_context(tc.manual_schedule())
+
+        bank_a = [ps.tile([P, BANK], F32, name="bank_a%d" % g) for g in range(G)]
+        bank_b = [ps.tile([P, BANK], F32, name="bank_b%d" % g) for g in range(G)]
+
+        def operand(name, width, dtype):
+            return {
+                "raw": sb.tile([P, PACK, width], dtype, name=name + "_raw", align_bytes=64),
+                "packed": sb.tile([P, width, PACK], BF16, name=name + "_packed", align_bytes=64),
+                "codes": sb.tile([P, width], U32, name=name + "_codes", align_bytes=64),
+                "scales": sb.tile([P, width], U8, name=name + "_scales", align_bytes=64),
+            }
+
+        def load(op, src):
+            nc.sync.dma_start(out=op["raw"][:], in_=src.rearrange("g (p j) c -> (g p) j c", j=PACK))
+
+        def pack(copy, op, lo=0, hi=None):
+            interleave(copy, op["packed"][:, lo:hi, :], op["raw"][:, :, lo:hi])
+
+        def quantize(op):
+            nc.vector.quantize_mx(
+                out=op["codes"][:].bitcast(FP8X4),
+                scales=op["scales"][:],
+                in_=op["packed"][:].rearrange("p c j -> p (c j)"),
+            )
+
+        def product(banks, col, wt, mv, width, groups):
+            for g in groups:
+                rows = slice(ROWS * g, ROWS * (g + 1))
+                for t in range(0, width, NT):
+                    nc.tensor.matmul_mx(
+                        out=banks[g][:, col + t : col + t + NT],
+                        lhsT=wt["codes"][rows, :].bitcast(FP8X4),
+                        lhsT_scale=wt["scales"][rows, :],
+                        rhs=mv["codes"][rows, t : t + NT].bitcast(FP8X4),
+                        rhs_scale=mv["scales"][rows, t : t + NT],
+                        start=True,
+                        stop=True,
+                    )
+
+        xs = [operand("x%d" % c, w, F32) for c, (s, w) in enumerate(CHUNKS)]
+        hq = [operand("h%d" % c, w, BF16) for c, (s, w) in enumerate(CHUNKS)]
+        q1 = operand("w1", M, F32)
+        q2 = operand("w2", M, F32)
+        q3 = operand("w3", M, F32)
+        qo = operand("wo", O, F32)
+        res_sb = sb.tile([P, G, N], F32, name="res_sb")
+        rows_in = sb.tile([P, 32], F32, name="rows_in", align_bytes=64)
+        cols = sb.tile([P, 32], F32, name="cols", align_bytes=64)
+        neg_th = sb.tile([P, 32], F32, name="neg_th", align_bytes=64)
+        warm_in = sb.tile([P, 8], F32, name="warm_in")
+        warm_out = sb.tile([P, 8], F32, name="warm_out")
+
+        def per_group(name, dtype):
+            return [
+                [sb.tile([P, w], dtype, name="%s_%d_%d" % (name, c, g), align_bytes=64) for g in range(G)]
+                for c, (s, w) in enumerate(CHUNKS)
+            ]
+
+        g2 = per_group("g2", F32)
+        g3 = per_group("g3", F32)
+        u = per_group("u", F32)
+        hh = per_group("hh", BF16)
+        y = [[sb.tile([P, 2, w], F32, name="y%d_%d" % (c, h)) for h in range(2)] for c, (s, w) in enumerate(CHUNKS)]
+
+        z2_at = [(bank_b, 0), (bank_a, 0), (bank_a, 0)]
+        z3_at = [(bank_a, 0), (bank_a, 128), (bank_a, 128)]
+        z1_at = [(bank_b, 256), (bank_b, 0), (bank_b, 0)]
+        y_at = [(bank_a, 0), (bank_b, 0), (bank_a, 256)]
+
+        def view(at, c, g):
+            banks, col = at[c]
+            return banks[g][:, col : col + CHUNKS[c][1]]
+
+        def mm(at, c, wt, mv, groups=range(G)):
+            product(at[c][0], at[c][1], wt, mv[c], CHUNKS[c][1], groups)
+
+        def mm_gates(c):
+            for g in range(G):
+                mm(z2_at, c, q2, xs, [g])
+                mm(z3_at, c, q3, xs, [g])
+
+        def sig2(c, g):
+            nc.scalar.activation(out=g2[c][g][:], in_=view(z2_at, c, g), func=ACT.Sigmoid)
+
+        def sig3(c, g):
+            nc.scalar.activation(
+                out=g3[c][g][:], in_=view(z3_at, c, g), func=ACT.Sigmoid, bias=neg_th[:, 8 * g : 8 * g + 1]
+            )
+
+        def gate2(c, g):
+            nc.vector.scalar_tensor_tensor(
+                out=u[c][g][:], in0=view(z1_at, c, g), scalar=cols[:, 8 * g + 4 : 8 * g + 5], in1=g2[c][g][:],
+                op0=ALU.mult, op1=ALU.mult,
+            )
+
+        def gate3(c, g):
+            nc.vector.tensor_tensor(out=hh[c][g][:], in0=u[c][g][:], in1=g3[c][g][:], op=ALU.mult)
+            nc.sync.dma_start(out=hq[c]["raw"][ROWS * g : ROWS * (g + 1), :, :], in_=hh[c][g][:])
+
+        def sigmoids(c):
+            sig2(c, 0)
+            for g in range(1, G):
+                sig2(c, g)
+                sig3(c, g - 1)
+            sig3(c, G - 1)
+
+        def gates(c):
+            gate2(c, 0)
+            for g in range(1, G):
+                gate2(c, g)
+                gate3(c, g - 1)
+            gate3(c, G - 1)
+
+        def finish(c, groups, queue):
+            s, w = CHUNKS[c]
+            for g in groups:
+                nc.vector.tensor_tensor(out=y[c][g // 2][:, g % 2, :], in0=view(y_at, c, g), in1=res_sb[:, g, s : s + w], op=ALU.add)
+                if g % 2 == 1:
+                    queue.dma_start(out=out[g - 1 : g + 1, :, s : s + w].rearrange("g o n -> o g n"), in_=y[c][g // 2][:])
+
+        def xcols(c):
+            s, w = CHUNKS[c]
+            return x[:, :, s : s + w]
+
+        nc.vector.memset(rows_in[:], 0.0)
+        nc.gpsimd.memset(warm_in[:], 0.0)
+        load(q2, w2)
+        load(xs[0], xcols(0))
+        nc.scalar.dma_start(out=rows_in[0:P:8, :], in_=th.rearrange("g (q a) o -> q g (a o)", a=32))
+        nc.scalar.dma_start(out=rows_in[4:P:8, :], in_=hs.rearrange("g (q a) o -> q g (a o)", a=32))
+        nc.scalar.activation(out=warm_out[:], in_=warm_in[:], func=ACT.Sigmoid)
+        load(q3, w3)
+        load(q1, w1)
+        load(xs[1], xcols(1))
+        load(xs[2], xcols(2))
+        load(qo, wo2)
+        nc.sync.dma_start(out=res_sb[:], in_=res.rearrange("g o n -> o g n"))
+
+        nc.vector.transpose(cols[:], rows_in[:])
+        pack(nc.scalar.copy, q2)
+        quantize(q2)
+        pack(nc.scalar.copy, xs[0], 0, 80)
+        pack(nc.vector.tensor_copy, xs[0], 80, 256)
+        nc.vector.tensor_scalar(out=neg_th[:], in0=cols[:], scalar1=-1.0, scalar2=None, op0=ALU.mult)
+        quantize(xs[0])
+        mm(z2_at, 0, q2, xs)
+        pack(nc.scalar.copy, q3)
+        pack(nc.vector.tensor_copy, q1)
+        quantize(q3)
+        quantize(q1)
+        mm(z3_at, 0, q3, xs)
+        for g in range(G):
+            sig2(0, g)
+        mm(z1_at, 0, q1, xs)
+        for g in range(G):
+            sig3(0, g)
+        pack(nc.vector.tensor_copy, xs[1])
+        gate2(0, 0)
+        quantize(xs[1])
+        mm_gates(1)
+        pack(nc.scalar.copy, xs[2])
+        for g in range(1, G):
+            gate2(0, g)
+            gate3(0, g - 1)
+        quantize(xs[2])
+        gate3(0, G - 1)
+        mm(z1_at, 1, q1, xs)
+        sigmoids(1)
+        gates(1)
+        mm_gates(2)
+        mm(z1_at, 2, q1, xs)
+        sigmoids(2)
+        gates(2)
+        pack(nc.scalar.copy, hq[0], 0, 128)
+        pack(nc.vector.tensor_copy, qo)
+        pack(nc.vector.tensor_copy, hq[0], 128, 256)
+        quantize(qo)
+        quantize(hq[0])
+        mm(y_at, 0, qo, hq)
+        pack(nc.scalar.copy, hq[1])
+        finish(0, [0, 1], nc.sync)
+        quantize(hq[1])
+        mm(y_at, 1, qo, hq)
+        finish(0, [2, 3], nc.sync)
+        pack(nc.scalar.copy, hq[2], 0, 48)
+        pack(nc.vector.tensor_copy, hq[2], 48, 128)
+        finish(1, [0], nc.sync)
+        quantize(hq[2])
+        mm(y_at, 2, qo, hq)
+        finish(1, [1, 2, 3], nc.sync)
+        finish(2, [0, 1], nc.scalar)
+        finish(2, [2, 3], nc.sync)

@@ -18,7 +18,7 @@ PACK = 4
 ROWS = 32
 NT = 128
 BANK = 512
-CHUNKS = [(0, 256), (256, 128), (384, 128)]
+CHUNKS = [(0, 128), (128, 128), (256, 128), (384, 128)]
 
 
 def interleave(copy, dst, src):
@@ -98,10 +98,10 @@ def tile_rows_ftwogates_kernel(tc, x, w1, w2, w3, th, hs, wo2, res, out):
         hh = per_group("hh", BF16)
         y = [[sb.tile([P, 2, w], F32, name="y%d_%d" % (c, h)) for h in range(2)] for c, (s, w) in enumerate(CHUNKS)]
 
-        z2_at = [(bank_b, 0), (bank_a, 0), (bank_a, 0)]
-        z3_at = [(bank_a, 0), (bank_a, 128), (bank_a, 128)]
-        z1_at = [(bank_b, 256), (bank_b, 0), (bank_b, 0)]
-        y_at = [(bank_a, 0), (bank_b, 0), (bank_a, 256)]
+        z2_at = [(bank_b, 0), (bank_b, 0), (bank_a, 0), (bank_b, 0)]
+        z3_at = [(bank_a, 128), (bank_b, 128), (bank_a, 128), (bank_b, 128)]
+        z1_at = [(bank_a, 256), (bank_b, 256), (bank_a, 256), (bank_a, 256)]
+        y_at = [(bank_b, 0), (bank_a, 0), (bank_b, 128), (bank_a, 128)]
 
         def view(at, c, g):
             banks, col = at[c]
@@ -110,10 +110,28 @@ def tile_rows_ftwogates_kernel(tc, x, w1, w2, w3, th, hs, wo2, res, out):
         def mm(at, c, wt, mv, groups=range(G)):
             product(at[c][0], at[c][1], wt, mv[c], CHUNKS[c][1], groups)
 
-        def mm_gates(c):
+        def mm_all(c):
             for g in range(G):
                 mm(z2_at, c, q2, xs, [g])
                 mm(z3_at, c, q3, xs, [g])
+                mm(z1_at, c, q1, xs, [g])
+
+        def mm_wide(c):
+            mm(z2_at, c, q2, xs)
+            mm(z3_at, c, q3, xs)
+            mm(z1_at, c, q1, xs)
+
+        def sigmoids(c):
+            for g in range(G):
+                sig2(c, g)
+                sig3(c, g)
+
+        def gates(c, eng=nc.vector):
+            gate2(c, 0)
+            for g in range(1, G):
+                gate2(c, g)
+                gate3(c, g - 1, eng)
+            gate3(c, G - 1, eng)
 
         def sig2(c, g):
             nc.scalar.activation(out=g2[c][g][:], in_=view(z2_at, c, g), func=ACT.Sigmoid)
@@ -129,23 +147,13 @@ def tile_rows_ftwogates_kernel(tc, x, w1, w2, w3, th, hs, wo2, res, out):
                 op0=ALU.mult, op1=ALU.mult,
             )
 
-        def gate3(c, g):
-            nc.vector.tensor_tensor(out=hh[c][g][:], in0=u[c][g][:], in1=g3[c][g][:], op=ALU.mult)
+        def gate3(c, g, eng=nc.vector):
+            eng.tensor_tensor(out=hh[c][g][:], in0=u[c][g][:], in1=g3[c][g][:], op=ALU.mult)
             nc.sync.dma_start(out=hq[c]["raw"][ROWS * g : ROWS * (g + 1), :, :], in_=hh[c][g][:])
 
-        def sigmoids(c):
-            sig2(c, 0)
-            for g in range(1, G):
-                sig2(c, g)
-                sig3(c, g - 1)
-            sig3(c, G - 1)
-
-        def gates(c):
-            gate2(c, 0)
-            for g in range(1, G):
-                gate2(c, g)
-                gate3(c, g - 1)
-            gate3(c, G - 1)
+        def each(f, c):
+            for g in range(G):
+                f(c, g)
 
         def finish(c, groups, queue):
             s, w = CHUNKS[c]
@@ -158,71 +166,80 @@ def tile_rows_ftwogates_kernel(tc, x, w1, w2, w3, th, hs, wo2, res, out):
             s, w = CHUNKS[c]
             return x[:, :, s : s + w]
 
-        nc.vector.memset(rows_in[:], 0.0)
+        nc.gpsimd.memset(rows_in[:], 0.0)
         nc.gpsimd.memset(warm_in[:], 0.0)
+        nc.scalar.activation(out=warm_out[:], in_=warm_in[:], func=ACT.Sigmoid)
         load(q2, w2)
         load(xs[0], xcols(0))
-        nc.scalar.dma_start(out=rows_in[0:P:8, :], in_=th.rearrange("g (q a) o -> q g (a o)", a=32))
-        nc.scalar.dma_start(out=rows_in[4:P:8, :], in_=hs.rearrange("g (q a) o -> q g (a o)", a=32))
-        nc.scalar.activation(out=warm_out[:], in_=warm_in[:], func=ACT.Sigmoid)
+        nc.sync.dma_start(out=rows_in[0:P:8, :], in_=th.rearrange("g (q a) o -> q g (a o)", a=32))
+        nc.sync.dma_start(out=rows_in[4:P:8, :], in_=hs.rearrange("g (q a) o -> q g (a o)", a=32))
         load(q3, w3)
         load(q1, w1)
         load(xs[1], xcols(1))
         load(xs[2], xcols(2))
         load(qo, wo2)
+        load(xs[3], xcols(3))
         nc.sync.dma_start(out=res_sb[:], in_=res.rearrange("g o n -> o g n"))
 
-        nc.vector.transpose(cols[:], rows_in[:])
         pack(nc.scalar.copy, q2)
+        pack(nc.vector.tensor_copy, xs[0])
         quantize(q2)
-        pack(nc.scalar.copy, xs[0], 0, 80)
-        pack(nc.vector.tensor_copy, xs[0], 80, 256)
-        nc.vector.tensor_scalar(out=neg_th[:], in0=cols[:], scalar1=-1.0, scalar2=None, op0=ALU.mult)
         quantize(xs[0])
         mm(z2_at, 0, q2, xs)
-        pack(nc.scalar.copy, q3)
-        pack(nc.vector.tensor_copy, q1)
+        pack(nc.vector.tensor_copy, q3)
+        nc.vector.transpose(cols[:], rows_in[:])
         quantize(q3)
-        quantize(q1)
+        nc.vector.tensor_scalar(out=neg_th[:], in0=cols[:], scalar1=-1.0, scalar2=None, op0=ALU.mult)
         mm(z3_at, 0, q3, xs)
-        for g in range(G):
-            sig2(0, g)
-        mm(z1_at, 0, q1, xs)
-        for g in range(G):
-            sig3(0, g)
+        pack(nc.scalar.copy, q1)
+        each(sig2, 0)
+        each(sig3, 0)
         pack(nc.vector.tensor_copy, xs[1])
-        gate2(0, 0)
+        quantize(q1)
         quantize(xs[1])
-        mm_gates(1)
-        pack(nc.scalar.copy, xs[2])
-        for g in range(1, G):
-            gate2(0, g)
-            gate3(0, g - 1)
+        mm_wide(1)
+        mm(z1_at, 0, q1, xs)
+        pack(nc.vector.tensor_copy, xs[2])
+        pack(nc.scalar.copy, qo)
         quantize(xs[2])
-        gate3(0, G - 1)
-        mm(z1_at, 1, q1, xs)
+        each(gate2, 0)
+        mm_wide(2)
         sigmoids(1)
-        gates(1)
-        mm_gates(2)
-        mm(z1_at, 2, q1, xs)
+        pack(nc.vector.tensor_copy, xs[3])
+        for g in range(G):
+            gate3(0, g, nc.vector)
+        quantize(xs[3])
+        each(gate2, 1)
+        mm(z2_at, 3, q2, xs)
+        mm(z3_at, 3, q3, xs)
         sigmoids(2)
-        gates(2)
-        pack(nc.scalar.copy, hq[0], 0, 128)
-        pack(nc.vector.tensor_copy, qo)
-        pack(nc.vector.tensor_copy, hq[0], 128, 256)
+        each(gate3, 1)
         quantize(qo)
+        each(gate2, 2)
+        mm(z1_at, 3, q1, xs)
+        each(gate3, 2)
+        sig2(3, 0)
+        for g in range(1, G):
+            sig2(3, g)
+            sig3(3, g - 1)
+        sig3(3, G - 1)
+        pack(nc.scalar.copy, hq[0])
+        pack(nc.scalar.copy, hq[1])
+        pack(nc.scalar.copy, hq[2])
+        gates(3)
         quantize(hq[0])
         mm(y_at, 0, qo, hq)
-        pack(nc.scalar.copy, hq[1])
-        finish(0, [0, 1], nc.sync)
         quantize(hq[1])
         mm(y_at, 1, qo, hq)
-        finish(0, [2, 3], nc.sync)
-        pack(nc.scalar.copy, hq[2], 0, 48)
-        pack(nc.vector.tensor_copy, hq[2], 48, 128)
-        finish(1, [0], nc.sync)
+        finish(0, range(G), nc.sync)
         quantize(hq[2])
         mm(y_at, 2, qo, hq)
-        finish(1, [1, 2, 3], nc.sync)
-        finish(2, [0, 1], nc.scalar)
-        finish(2, [2, 3], nc.sync)
+        finish(1, [0, 1], nc.sync)
+        pack(nc.scalar.copy, hq[3], 0, 48)
+        pack(nc.vector.tensor_copy, hq[3], 48, 128)
+        finish(1, [2, 3], nc.sync)
+        quantize(hq[3])
+        mm(y_at, 3, qo, hq)
+        finish(2, range(G), nc.sync)
+        finish(3, [0, 1], nc.scalar)
+        finish(3, [2, 3], nc.sync)

@@ -18,14 +18,15 @@ PACK = 4
 ROWS = 32
 NT = 128
 BANK = 512
-CHUNKS = [(0, 128), (128, 128), (256, 128), (384, 128)]
+CHUNKS = N // NT
+X_PIECES = [(0, 128), (128, 128), (256, 128), (384, 128)]
+H_PIECES = [(0, 128), (128, 128), (256, 128), (384, 128)]
 
 
-def interleave(copy, dst, src):
-    copy(
-        out=dst.rearrange("p (c i) j -> p c j i", i=4),
-        in_=src.rearrange("p j (c i) -> p c j i", i=4),
-    )
+def piece_of(pieces, c):
+    for i, (s, w) in enumerate(pieces):
+        if s <= c * NT < s + w:
+            return i, c * NT - s
 
 
 def tile_rows_ftwogates_kernel(tc, x, w1, w2, w3, th, hs, wo2, res, out):
@@ -46,11 +47,14 @@ def tile_rows_ftwogates_kernel(tc, x, w1, w2, w3, th, hs, wo2, res, out):
                 "scales": sb.tile([P, width], U8, name=name + "_scales", align_bytes=64),
             }
 
-        def load(op, src):
-            nc.sync.dma_start(out=op["raw"][:], in_=src.rearrange("g (p j) c -> (g p) j c", j=PACK))
+        def load(op, src, queue=nc.sync):
+            queue.dma_start(out=op["raw"][:], in_=src.rearrange("g (p j) c -> (g p) j c", j=PACK))
 
         def pack(copy, op, lo=0, hi=None):
-            interleave(copy, op["packed"][:, lo:hi, :], op["raw"][:, :, lo:hi])
+            copy(
+                out=op["packed"][:, lo:hi, :].rearrange("p (c i) j -> p c j i", i=4),
+                in_=op["raw"][:, :, lo:hi].rearrange("p j (c i) -> p c j i", i=4),
+            )
 
         def quantize(op):
             nc.vector.quantize_mx(
@@ -59,22 +63,21 @@ def tile_rows_ftwogates_kernel(tc, x, w1, w2, w3, th, hs, wo2, res, out):
                 in_=op["packed"][:].rearrange("p c j -> p (c j)"),
             )
 
-        def product(banks, col, wt, mv, width, groups):
+        def product(banks, col, wt, mv, t, groups=range(G)):
             for g in groups:
                 rows = slice(ROWS * g, ROWS * (g + 1))
-                for t in range(0, width, NT):
-                    nc.tensor.matmul_mx(
-                        out=banks[g][:, col + t : col + t + NT],
-                        lhsT=wt["codes"][rows, :].bitcast(FP8X4),
-                        lhsT_scale=wt["scales"][rows, :],
-                        rhs=mv["codes"][rows, t : t + NT].bitcast(FP8X4),
-                        rhs_scale=mv["scales"][rows, t : t + NT],
-                        start=True,
-                        stop=True,
-                    )
+                nc.tensor.matmul_mx(
+                    out=banks[g][:, col : col + NT],
+                    lhsT=wt["codes"][rows, :].bitcast(FP8X4),
+                    lhsT_scale=wt["scales"][rows, :],
+                    rhs=mv["codes"][rows, t : t + NT].bitcast(FP8X4),
+                    rhs_scale=mv["scales"][rows, t : t + NT],
+                    start=True,
+                    stop=True,
+                )
 
-        xs = [operand("x%d" % c, w, F32) for c, (s, w) in enumerate(CHUNKS)]
-        hq = [operand("h%d" % c, w, BF16) for c, (s, w) in enumerate(CHUNKS)]
+        xs = [operand("x%d" % i, w, F32) for i, (s, w) in enumerate(X_PIECES)]
+        hq = [operand("h%d" % i, w, BF16) for i, (s, w) in enumerate(H_PIECES)]
         q1 = operand("w1", M, F32)
         q2 = operand("w2", M, F32)
         q3 = operand("w3", M, F32)
@@ -86,52 +89,38 @@ def tile_rows_ftwogates_kernel(tc, x, w1, w2, w3, th, hs, wo2, res, out):
         warm_in = sb.tile([P, 8], F32, name="warm_in")
         warm_out = sb.tile([P, 8], F32, name="warm_out")
 
-        def per_group(name, dtype):
-            return [
-                [sb.tile([P, w], dtype, name="%s_%d_%d" % (name, c, g), align_bytes=64) for g in range(G)]
-                for c, (s, w) in enumerate(CHUNKS)
-            ]
+        def per_group(name):
+            return [[sb.tile([P, NT], F32, name="%s_%d_%d" % (name, c, g)) for g in range(G)] for c in range(CHUNKS)]
 
-        g2 = per_group("g2", F32)
-        g3 = per_group("g3", F32)
-        u = per_group("u", F32)
-        hh = per_group("hh", BF16)
-        y = [[sb.tile([P, 2, w], F32, name="y%d_%d" % (c, h)) for h in range(2)] for c, (s, w) in enumerate(CHUNKS)]
+        g2 = per_group("g2")
+        g3 = per_group("g3")
+        u = per_group("u")
+        hh = [[sb.tile([P, w], BF16, name="hh_%d_%d" % (i, g)) for g in range(G)] for i, (s, w) in enumerate(H_PIECES)]
+        y = [[sb.tile([P, w], F32, name="y_%d_%d" % (i, g)) for g in range(G)] for i, (s, w) in enumerate(H_PIECES)]
+        y2 = [[sb.tile([P, 2, w], F32, name="yy_%d_%d" % (i, h)) for h in range(2)] for i, (s, w) in enumerate(H_PIECES)]
 
         z2_at = [(bank_b, 0), (bank_b, 0), (bank_a, 0), (bank_b, 0)]
         z3_at = [(bank_a, 128), (bank_b, 128), (bank_a, 128), (bank_b, 128)]
         z1_at = [(bank_a, 256), (bank_b, 256), (bank_a, 256), (bank_a, 256)]
         y_at = [(bank_b, 0), (bank_a, 0), (bank_b, 128), (bank_a, 128)]
 
-        def view(at, c, g):
+        def view(at, c, g, w=NT):
             banks, col = at[c]
-            return banks[g][:, col : col + CHUNKS[c][1]]
+            return banks[g][:, col : col + w]
 
-        def mm(at, c, wt, mv, groups=range(G)):
-            product(at[c][0], at[c][1], wt, mv[c], CHUNKS[c][1], groups)
-
-        def mm_all(c):
-            for g in range(G):
-                mm(z2_at, c, q2, xs, [g])
-                mm(z3_at, c, q3, xs, [g])
-                mm(z1_at, c, q1, xs, [g])
+        def mm(at, c, wt, groups=range(G)):
+            i, t = piece_of(X_PIECES, c)
+            product(at[c][0], at[c][1], wt, xs[i], t, groups)
 
         def mm_wide(c):
-            mm(z2_at, c, q2, xs)
-            mm(z3_at, c, q3, xs)
-            mm(z1_at, c, q1, xs)
+            for pair in ([0, 1], [2, 3]):
+                mm(z2_at, c, q2, pair)
+                mm(z3_at, c, q3, pair)
+                mm(z1_at, c, q1, pair)
 
-        def sigmoids(c):
-            for g in range(G):
-                sig2(c, g)
-                sig3(c, g)
-
-        def gates(c, eng=nc.vector):
-            gate2(c, 0)
-            for g in range(1, G):
-                gate2(c, g)
-                gate3(c, g - 1, eng)
-            gate3(c, G - 1, eng)
+        def mm_out(i):
+            for t in range(0, H_PIECES[i][1], NT):
+                product(y_at[i][0], y_at[i][1] + t, qo, hq[i], t)
 
         def sig2(c, g):
             nc.scalar.activation(out=g2[c][g][:], in_=view(z2_at, c, g), func=ACT.Sigmoid)
@@ -148,98 +137,128 @@ def tile_rows_ftwogates_kernel(tc, x, w1, w2, w3, th, hs, wo2, res, out):
             )
 
         def gate3(c, g, eng=nc.vector):
-            eng.tensor_tensor(out=hh[c][g][:], in0=u[c][g][:], in1=g3[c][g][:], op=ALU.mult)
-            nc.sync.dma_start(out=hq[c]["raw"][ROWS * g : ROWS * (g + 1), :, :], in_=hh[c][g][:])
+            i, t = piece_of(H_PIECES, c)
+            eng.tensor_tensor(out=hh[i][g][:, t : t + NT], in0=u[c][g][:], in1=g3[c][g][:], op=ALU.mult)
+            if t + NT == H_PIECES[i][1]:
+                nc.sync.dma_start(out=hq[i]["raw"][ROWS * g : ROWS * (g + 1), :, :], in_=hh[i][g][:])
 
         def each(f, c):
             for g in range(G):
                 f(c, g)
 
-        def finish(c, groups, queue):
-            s, w = CHUNKS[c]
-            for g in groups:
-                nc.vector.tensor_tensor(out=y[c][g // 2][:, g % 2, :], in0=view(y_at, c, g), in1=res_sb[:, g, s : s + w], op=ALU.add)
-                if g % 2 == 1:
-                    queue.dma_start(out=out[g - 1 : g + 1, :, s : s + w].rearrange("g o n -> o g n"), in_=y[c][g // 2][:])
+        def sigmoids(c):
+            for g in range(G):
+                sig2(c, g)
+                sig3(c, g)
 
-        def xcols(c):
-            s, w = CHUNKS[c]
-            return x[:, :, s : s + w]
+        def staggered(first, second, c):
+            first(c, 0)
+            for g in range(1, G):
+                first(c, g)
+                second(c, g - 1)
+            second(c, G - 1)
+
+        def finish(i, groups, queue):
+            s, w = H_PIECES[i]
+            for g in groups:
+                nc.vector.tensor_tensor(out=y2[i][g // 2][:, g % 2, :], in0=view(y_at, i, g, w), in1=res_sb[:, g, s : s + w], op=ALU.add)
+                if g % 2 == 1:
+                    queue.dma_start(out=out[g - 1 : g + 1, :, s : s + w].rearrange("g o n -> o g n"), in_=y2[i][g // 2][:])
+
+        def finish1(i, g, queue):
+            s, w = H_PIECES[i]
+            nc.vector.tensor_tensor(out=y[i][g][:], in0=view(y_at, i, g, w), in1=res_sb[:, g, s : s + w], op=ALU.add)
+            queue.dma_start(out=out[g, :, s : s + w], in_=y[i][g][:])
+
+        def load_x(i, queue=nc.sync):
+            s, w = X_PIECES[i]
+            load(xs[i], x[:, :, s : s + w], queue)
+
+        V = nc.vector.tensor_copy
+        A = nc.scalar.copy
 
         nc.gpsimd.memset(rows_in[:], 0.0)
         nc.gpsimd.memset(warm_in[:], 0.0)
         nc.scalar.activation(out=warm_out[:], in_=warm_in[:], func=ACT.Sigmoid)
         load(q2, w2)
-        load(xs[0], xcols(0))
+        load_x(0)
         nc.sync.dma_start(out=rows_in[0:P:8, :], in_=th.rearrange("g (q a) o -> q g (a o)", a=32))
         nc.sync.dma_start(out=rows_in[4:P:8, :], in_=hs.rearrange("g (q a) o -> q g (a o)", a=32))
         load(q3, w3)
         load(q1, w1)
-        load(xs[1], xcols(1))
-        load(xs[2], xcols(2))
+        load_x(1)
+        load_x(2)
         load(qo, wo2)
-        load(xs[3], xcols(3))
-        nc.sync.dma_start(out=res_sb[:], in_=res.rearrange("g o n -> o g n"))
+        load_x(3)
+        nc.sync.dma_start(out=res_sb[:, 0:2, :], in_=res[0:2].rearrange("g o n -> o g n"))
 
-        pack(nc.scalar.copy, q2)
-        pack(nc.vector.tensor_copy, xs[0])
+        pack(A, q2)
+        pack(V, xs[0])
         quantize(q2)
         quantize(xs[0])
-        mm(z2_at, 0, q2, xs)
-        pack(nc.vector.tensor_copy, q3)
+        mm(z2_at, 0, q2)
+        pack(V, q3)
         nc.vector.transpose(cols[:], rows_in[:])
         quantize(q3)
+        pack(V, q1)
         nc.vector.tensor_scalar(out=neg_th[:], in0=cols[:], scalar1=-1.0, scalar2=None, op0=ALU.mult)
-        mm(z3_at, 0, q3, xs)
-        pack(nc.scalar.copy, q1)
-        each(sig2, 0)
-        each(sig3, 0)
-        pack(nc.vector.tensor_copy, xs[1])
         quantize(q1)
+        mm(z3_at, 0, q3)
+        mm(z1_at, 0, q1)
+        each(sig2, 0)
+        pack(V, xs[1])
+        each(sig3, 0)
         quantize(xs[1])
         mm_wide(1)
-        mm(z1_at, 0, q1, xs)
-        pack(nc.vector.tensor_copy, xs[2])
-        pack(nc.scalar.copy, qo)
+        pack(V, xs[2])
+        pack(A, qo)
+        gate2(0, 0)
         quantize(xs[2])
-        each(gate2, 0)
+        for g in range(1, G):
+            gate2(0, g)
         mm_wide(2)
         sigmoids(1)
-        pack(nc.vector.tensor_copy, xs[3])
-        for g in range(G):
-            gate3(0, g, nc.vector)
+        pack(V, xs[3])
+        each(gate3, 0)
+        nc.sync.dma_start(out=res_sb[:, 2:4, :], in_=res[2:4].rearrange("g o n -> o g n"))
         quantize(xs[3])
         each(gate2, 1)
-        mm(z2_at, 3, q2, xs)
-        mm(z3_at, 3, q3, xs)
+        for pair in ([0, 1], [2, 3]):
+            mm(z2_at, 3, q2, pair)
+            mm(z3_at, 3, q3, pair)
         sigmoids(2)
         each(gate3, 1)
-        quantize(qo)
         each(gate2, 2)
-        mm(z1_at, 3, q1, xs)
+        mm(z1_at, 3, q1)
         each(gate3, 2)
-        sig2(3, 0)
-        for g in range(1, G):
-            sig2(3, g)
-            sig3(3, g - 1)
-        sig3(3, G - 1)
-        pack(nc.scalar.copy, hq[0])
-        pack(nc.scalar.copy, hq[1])
-        pack(nc.scalar.copy, hq[2])
-        gates(3)
+        staggered(sig2, sig3, 3)
+        pack(A, hq[0])
+        pack(A, hq[1])
+        pack(A, hq[2])
+        gate2(3, 0)
+        gate2(3, 1)
+        quantize(qo)
+        gate3(3, 0)
+        gate2(3, 2)
+        gate3(3, 1)
+        gate2(3, 3)
+        gate3(3, 2)
+        gate3(3, 3)
         quantize(hq[0])
-        mm(y_at, 0, qo, hq)
+        mm_out(0)
         quantize(hq[1])
-        mm(y_at, 1, qo, hq)
+        mm_out(1)
         finish(0, range(G), nc.sync)
         quantize(hq[2])
-        mm(y_at, 2, qo, hq)
+        mm_out(2)
         finish(1, [0, 1], nc.sync)
-        pack(nc.scalar.copy, hq[3], 0, 48)
-        pack(nc.vector.tensor_copy, hq[3], 48, 128)
+        pack(A, hq[3], 0, 48)
+        pack(V, hq[3], 48, 128)
         finish(1, [2, 3], nc.sync)
         quantize(hq[3])
-        mm(y_at, 3, qo, hq)
+        mm_out(3)
         finish(2, range(G), nc.sync)
-        finish(3, [0, 1], nc.scalar)
-        finish(3, [2, 3], nc.sync)
+        finish1(3, 0, nc.scalar)
+        finish1(3, 1, nc.sync)
+        finish1(3, 2, nc.scalar)
+        finish1(3, 3, nc.sync)

from contextlib import ExitStack

import concourse.mybir as mybir

G, D, M, O, N = 4, 128, 128, 128, 512
FLOPS = 2 * G * N * (3 * D * M + M * O)

F32 = mybir.dt.float32
BF16 = mybir.dt.bfloat16
U32 = mybir.dt.uint32
U8 = mybir.dt.uint8
FP8X4 = mybir.dt.float8_e4m3fn_x4
ALU = mybir.AluOpType
ACT = mybir.ActivationFunctionType

P = 128
PACK = 4
ROWS = 32
NT = 128
BANK = 512
CHUNKS = N // NT
X_PIECES = [(0, 128), (128, 128), (256, 128), (384, 128)]
H_PIECES = [(0, 128), (128, 128), (256, 128), (384, 128)]


def piece_of(pieces, c):
    for i, (s, w) in enumerate(pieces):
        if s <= c * NT < s + w:
            return i, c * NT - s


def tile_rows_ftwogates_kernel(tc, x, w1, w2, w3, th, hs, wo2, res, out):
    nc = tc.nc
    with ExitStack() as ctx:
        sb = ctx.enter_context(tc.tile_pool(name="sb", bufs=1))
        ps = ctx.enter_context(tc.psum_pool(name="ps", bufs=1))
        ctx.enter_context(tc.manual_schedule())

        bank_a = [ps.tile([P, BANK], F32, name="bank_a%d" % g) for g in range(G)]
        bank_b = [ps.tile([P, BANK], F32, name="bank_b%d" % g) for g in range(G)]

        def operand(name, width, dtype):
            return {
                "raw": sb.tile([P, PACK, width], dtype, name=name + "_raw", align_bytes=64),
                "packed": sb.tile([P, width, PACK], BF16, name=name + "_packed", align_bytes=64),
                "codes": sb.tile([P, width], U32, name=name + "_codes", align_bytes=64),
                "scales": sb.tile([P, width], U8, name=name + "_scales", align_bytes=64),
            }

        def load(op, src, queue=nc.sync):
            queue.dma_start(out=op["raw"][:], in_=src.rearrange("g (p j) c -> (g p) j c", j=PACK))

        def pack(copy, op, lo=0, hi=None):
            copy(
                out=op["packed"][:, lo:hi, :].rearrange("p (c i) j -> p c j i", i=4),
                in_=op["raw"][:, :, lo:hi].rearrange("p j (c i) -> p c j i", i=4),
            )

        def quantize(op):
            nc.vector.quantize_mx(
                out=op["codes"][:].bitcast(FP8X4),
                scales=op["scales"][:],
                in_=op["packed"][:].rearrange("p c j -> p (c j)"),
            )

        def product(banks, col, wt, mv, t, groups=range(G)):
            for g in groups:
                rows = slice(ROWS * g, ROWS * (g + 1))
                nc.tensor.matmul_mx(
                    out=banks[g][:, col : col + NT],
                    lhsT=wt["codes"][rows, :].bitcast(FP8X4),
                    lhsT_scale=wt["scales"][rows, :],
                    rhs=mv["codes"][rows, t : t + NT].bitcast(FP8X4),
                    rhs_scale=mv["scales"][rows, t : t + NT],
                    start=True,
                    stop=True,
                )

        xs = [operand("x%d" % i, w, F32) for i, (s, w) in enumerate(X_PIECES)]
        hq = [operand("h%d" % i, w, BF16) for i, (s, w) in enumerate(H_PIECES)]
        q1 = operand("w1", M, F32)
        q2 = operand("w2", M, F32)
        q3 = operand("w3", M, F32)
        qo = operand("wo", O, F32)
        res_sb = sb.tile([P, G, N], F32, name="res_sb")
        rows_in = sb.tile([P, 32], F32, name="rows_in", align_bytes=64)
        cols = sb.tile([P, 32], F32, name="cols", align_bytes=64)
        neg_th = sb.tile([P, 32], F32, name="neg_th", align_bytes=64)
        warm_in = sb.tile([P, 8], F32, name="warm_in")
        warm_out = sb.tile([P, 8], F32, name="warm_out")

        def per_group(name):
            return [[sb.tile([P, NT], F32, name="%s_%d_%d" % (name, c, g)) for g in range(G)] for c in range(CHUNKS)]

        g2 = per_group("g2")
        g3 = per_group("g3")
        u = per_group("u")
        hh = [[sb.tile([P, w], BF16, name="hh_%d_%d" % (i, g)) for g in range(G)] for i, (s, w) in enumerate(H_PIECES)]
        y = [[sb.tile([P, w], F32, name="y_%d_%d" % (i, g)) for g in range(G)] for i, (s, w) in enumerate(H_PIECES)]
        y2 = [[sb.tile([P, 2, w], F32, name="yy_%d_%d" % (i, h)) for h in range(2)] for i, (s, w) in enumerate(H_PIECES)]

        z2_at = [(bank_b, 0), (bank_b, 0), (bank_a, 0), (bank_b, 0)]
        z3_at = [(bank_a, 128), (bank_b, 128), (bank_a, 128), (bank_b, 128)]
        z1_at = [(bank_a, 256), (bank_b, 256), (bank_a, 256), (bank_a, 256)]
        y_at = [(bank_b, 0), (bank_a, 0), (bank_b, 128), (bank_a, 128)]

        def view(at, c, g, w=NT):
            banks, col = at[c]
            return banks[g][:, col : col + w]

        def mm(at, c, wt, groups=range(G)):
            i, t = piece_of(X_PIECES, c)
            product(at[c][0], at[c][1], wt, xs[i], t, groups)

        def mm_wide(c):
            for pair in ([0, 1], [2, 3]):
                mm(z2_at, c, q2, pair)
                mm(z3_at, c, q3, pair)
                mm(z1_at, c, q1, pair)

        def mm_out(i):
            for t in range(0, H_PIECES[i][1], NT):
                product(y_at[i][0], y_at[i][1] + t, qo, hq[i], t)

        def sig2(c, g):
            nc.scalar.activation(out=g2[c][g][:], in_=view(z2_at, c, g), func=ACT.Sigmoid)

        def sig3(c, g):
            nc.scalar.activation(
                out=g3[c][g][:], in_=view(z3_at, c, g), func=ACT.Sigmoid, bias=neg_th[:, 8 * g : 8 * g + 1]
            )

        def gate2(c, g):
            nc.vector.scalar_tensor_tensor(
                out=u[c][g][:], in0=view(z1_at, c, g), scalar=cols[:, 8 * g + 4 : 8 * g + 5], in1=g2[c][g][:],
                op0=ALU.mult, op1=ALU.mult,
            )

        def gate3(c, g, eng=nc.vector):
            i, t = piece_of(H_PIECES, c)
            eng.tensor_tensor(out=hh[i][g][:, t : t + NT], in0=u[c][g][:], in1=g3[c][g][:], op=ALU.mult)
            if t + NT == H_PIECES[i][1]:
                nc.sync.dma_start(out=hq[i]["raw"][ROWS * g : ROWS * (g + 1), :, :], in_=hh[i][g][:])

        def each(f, c):
            for g in range(G):
                f(c, g)

        def sigmoids(c):
            for g in range(G):
                sig2(c, g)
                sig3(c, g)

        def staggered(first, second, c):
            first(c, 0)
            for g in range(1, G):
                first(c, g)
                second(c, g - 1)
            second(c, G - 1)

        def finish(i, groups, queue):
            s, w = H_PIECES[i]
            for g in groups:
                nc.vector.tensor_tensor(out=y2[i][g // 2][:, g % 2, :], in0=view(y_at, i, g, w), in1=res_sb[:, g, s : s + w], op=ALU.add)
                if g % 2 == 1:
                    queue.dma_start(out=out[g - 1 : g + 1, :, s : s + w].rearrange("g o n -> o g n"), in_=y2[i][g // 2][:])

        def finish1(i, g, queue):
            s, w = H_PIECES[i]
            nc.vector.tensor_tensor(out=y[i][g][:], in0=view(y_at, i, g, w), in1=res_sb[:, g, s : s + w], op=ALU.add)
            queue.dma_start(out=out[g, :, s : s + w], in_=y[i][g][:])

        def load_x(i, queue=nc.sync):
            s, w = X_PIECES[i]
            load(xs[i], x[:, :, s : s + w], queue)

        V = nc.vector.tensor_copy
        A = nc.scalar.copy

        nc.gpsimd.memset(rows_in[:], 0.0)
        nc.gpsimd.memset(warm_in[:], 0.0)
        nc.scalar.activation(out=warm_out[:], in_=warm_in[:], func=ACT.Sigmoid)
        load(q2, w2)
        load_x(0)
        nc.sync.dma_start(out=rows_in[0:P:8, :], in_=th.rearrange("g (q a) o -> q g (a o)", a=32))
        nc.sync.dma_start(out=rows_in[4:P:8, :], in_=hs.rearrange("g (q a) o -> q g (a o)", a=32))
        load(q3, w3)
        load(q1, w1)
        load_x(1)
        load_x(2)
        load(qo, wo2)
        load_x(3)
        nc.sync.dma_start(out=res_sb[:, 0:2, :], in_=res[0:2].rearrange("g o n -> o g n"))

        pack(A, q2)
        pack(V, xs[0])
        quantize(q2)
        quantize(xs[0])
        mm(z2_at, 0, q2)
        pack(V, q3)
        nc.vector.transpose(cols[:], rows_in[:])
        quantize(q3)
        pack(V, q1)
        nc.vector.tensor_scalar(out=neg_th[:], in0=cols[:], scalar1=-1.0, scalar2=None, op0=ALU.mult)
        quantize(q1)
        mm(z3_at, 0, q3)
        mm(z1_at, 0, q1)
        each(sig2, 0)
        pack(V, xs[1])
        each(sig3, 0)
        quantize(xs[1])
        mm_wide(1)
        pack(V, xs[2])
        pack(A, qo)
        gate2(0, 0)
        quantize(xs[2])
        for g in range(1, G):
            gate2(0, g)
        mm_wide(2)
        sigmoids(1)
        pack(V, xs[3])
        each(gate3, 0)
        nc.sync.dma_start(out=res_sb[:, 2:4, :], in_=res[2:4].rearrange("g o n -> o g n"))
        quantize(xs[3])
        each(gate2, 1)
        for pair in ([0, 1], [2, 3]):
            mm(z2_at, 3, q2, pair)
            mm(z3_at, 3, q3, pair)
        sigmoids(2)
        each(gate3, 1)
        each(gate2, 2)
        mm(z1_at, 3, q1)
        each(gate3, 2)
        staggered(sig2, sig3, 3)
        pack(A, hq[0])
        pack(A, hq[1])
        pack(A, hq[2])
        gate2(3, 0)
        gate2(3, 1)
        quantize(qo)
        gate3(3, 0)
        gate2(3, 2)
        gate3(3, 1)
        gate2(3, 3)
        gate3(3, 2)
        gate3(3, 3)
        quantize(hq[0])
        mm_out(0)
        quantize(hq[1])
        mm_out(1)
        finish(0, range(G), nc.sync)
        quantize(hq[2])
        mm_out(2)
        finish(1, [0, 1], nc.sync)
        pack(A, hq[3], 0, 48)
        pack(V, hq[3], 48, 128)
        finish(1, [2, 3], nc.sync)
        quantize(hq[3])
        mm_out(3)
        finish(2, range(G), nc.sync)
        finish1(3, 0, nc.scalar)
        finish1(3, 1, nc.sync)
        finish1(3, 2, nc.scalar)
        finish1(3, 3, nc.sync)
